import numpy as np
import ml_dtypes


def mxq(x, axis, fmt="e4m3"):
    dtype, down = {"e4m3": (ml_dtypes.float8_e4m3fn, 7), "e5m2": (ml_dtypes.float8_e5m2, 14)}[fmt]
    v = np.moveaxis(np.asarray(x, np.float32).astype(ml_dtypes.bfloat16).astype(np.float64), axis, -1)
    blocks = v.reshape(v.shape[:-1] + (-1, 32))
    amax = np.abs(blocks).max(-1, keepdims=True)
    byte = np.maximum(np.where(amax > 0, np.frexp(amax)[1] - 1 + 127, 0) - down, 1)
    scale = np.exp2(byte - 127.0)
    codes = (blocks / scale).astype(np.float32).astype(dtype).astype(np.float64)
    return np.moveaxis((codes * scale).reshape(v.shape), -1, axis)


WIDE = False


def mx_kscale(k):
    if not WIDE:
        return np.ones(k)
    levels = np.array([10, -10, 5, -5, 0])
    if k % 512:
        return np.exp2(np.random.permutation(np.resize(levels, k // 32))).repeat(32)
    a = np.empty((k // 512, 16))
    for p in range(k // 512):
        a[p, :8] = np.random.permutation(np.resize(levels, 8))
        for g in range(8):
            far = levels[np.abs(levels - a[p, g]) >= 10]
            a[p, g + 8] = far[np.random.randint(len(far))]
    return np.exp2(a.ravel()).repeat(32)


def f64(x):
    return np.asarray(x).astype(np.float64)


def striped(idx):
    return np.tile(np.asarray(idx).reshape(-1, 16).T, (8, 1)).astype(np.uint16)


def unstriped(offs):
    return offs[:16].T.reshape(-1).astype(np.int64)


E2M1 = np.array([0.0, 0.5, 1.0, 1.5, 2.0, 3.0, 4.0, 6.0, -0.0, -0.5, -1.0, -1.5, -2.0, -3.0, -4.0, -6.0])


def pack_weight(w, fmt):
    k, n = w.shape
    w = f64(np.asarray(w, np.float32).astype(ml_dtypes.bfloat16)).reshape(k // 32, 32, n)
    amax = np.abs(w).max(1)
    if fmt == "e4m3":
        byte = np.frexp(amax)[1] - 1 + 127 - 7
    else:
        mant, ex = np.frexp(amax / 6.0)
        byte = np.where(mant > 0.5, ex, ex - 1) + 127
    byte = np.clip(np.where(amax > 0, byte, 1), 1, 254)
    scaled = (w * np.exp2(127.0 - byte)[:, None, :]).reshape(k, n).astype(np.float32)
    by_word = np.ascontiguousarray(scaled.reshape(k // 512, 128, 4, n).transpose(0, 1, 3, 2))
    if fmt == "e4m3":
        words = by_word.astype(ml_dtypes.float8_e4m3fn).view(np.uint8)
    else:
        c = by_word.astype(ml_dtypes.float4_e2m1fn).view(np.uint8) & 0xF
        words = (c[..., 0::2] | (c[..., 1::2] << 4)).reshape(k // 512, 128, 2 * n)
    return np.ascontiguousarray(words), np.ascontiguousarray(byte.astype(np.uint8).reshape(k // 512, 16, n))


def unpack_weight(words, scales, fmt):
    g, _, n = scales.shape
    words = np.ascontiguousarray(words).reshape(g, 128, n, -1)
    if fmt == "e4m3":
        vals = words.view(ml_dtypes.float8_e4m3fn).astype(np.float64)
    else:
        nib = np.empty((g, 128, n, 4), np.uint8)
        nib[..., 0::2] = words & 0xF
        nib[..., 1::2] = words >> 4
        vals = E2M1[nib]
    vals = vals * np.repeat(np.exp2(scales.astype(np.float64) - 127.0), 8, axis=1)[..., None]
    return vals.transpose(0, 1, 3, 2).reshape(g * 512, n)


D, E, T, I, Q = 512, 512, 2048, 512, 128


def setup_inputs():
    n = np.random.standard_normal
    idx2 = np.random.permutation(I)[:I]
    idx = np.random.permutation(T)[:I]
    fd = mx_kscale(D)
    fe = mx_kscale(E)
    keysp = pack_weight(n((D, T)) / fd[:, None], "e2m1")
    valsp = pack_weight(n((E, T)) / fe[:, None], "e2m1")
    return {
        "query": (n((D, Q)) * 0.8 / np.sqrt(D) * fd[:, None]).astype(np.float32),
        "keys_words": keysp[0],
        "keys_scales": keysp[1],
        "reserve": (np.random.uniform(0.5, 2.0, (Q, 1))).astype(np.float32),
        "gout": (n((E, Q)) * 1 / np.sqrt(E) * fe[:, None]).astype(np.float32),
        "vals_words": valsp[0],
        "vals_scales": valsp[1],
        "old": (0.5 * n((Q, T))).astype(np.float32),
        "offs2": striped(idx2),
        "offs": striped(idx),
    }


def reference(query, keys_words, keys_scales, reserve, gout, vals_words, vals_scales, old, offs2, offs):
    idx2 = unstriped(offs2)
    idx = unstriped(offs)
    keysu = unpack_weight(keys_words, keys_scales, "e2m1")
    valsu = unpack_weight(vals_words, vals_scales, "e2m1")
    queryq = mxq(f64(query), 0, "e4m3")
    keysidxg = keysu[:, idx]
    a = queryq.T @ keysidxg
    p = np.exp(a)
    z = np.sum(p, axis=1, keepdims=True)
    r = p / (p + p[:, idx2] + f64(reserve))
    goutq = mxq(f64(gout), 0, "e4m3")
    valsidxg = valsu[:, idx]
    c0 = goutq.T @ valsidxg
    dr = c0 * p / z
    dz = np.sum(c0 * r * p / np.square(z) * (-1.0), axis=1, keepdims=True)
    e1 = dr * p / np.square(p + p[:, idx2] + f64(reserve)) * (-1.0)
    s1 = np.zeros((Q, I))
    s1[:, idx2] = e1
    dp = c0 * r / z + dr / (p + p[:, idx2] + f64(reserve)) + dz + s1 - dr * p / np.square(p + p[:, idx2] + f64(reserve))
    da = dp * p
    gs = da * 512.0
    gf = np.zeros((Q, T))
    gf[:, idx] = gs
    y = f64(old) + gf
    return y

@@ -1,0 +1,157 @@
+from contextlib import ExitStack
+
+import concourse.mybir as mybir
+
+F32 = mybir.dt.float32
+BF16 = mybir.dt.bfloat16
+I32 = mybir.dt.int32
+U32 = mybir.dt.uint32
+U16 = mybir.dt.uint16
+U8 = mybir.dt.uint8
+FP8X4 = mybir.dt.float8_e4m3fn_x4
+FP4X4 = mybir.dt.float4_e2m1fn_x4
+ALU = mybir.AluOpType
+ACT = mybir.ActivationFunctionType
+
+P = 128
+PACK = 4
+T = 2048
+SLOTS = 512
+ROWS = 128
+HALF = SLOTS // 2
+LIST_COLS = HALF // 16
+GAIN = 512.0
+OUT_CHUNKS = (640, 640, 512, 256)
+
+FLOPS = 2 * 2 * 512 * ROWS * SLOTS
+
+
+def tile_attend_bneighbourshare_s_kernel(tc, query, keys_words, keys_scales, reserve, gout, vals_words, vals_scales, old, offs2, offs, out):
+    nc = tc.nc
+    with ExitStack() as ctx:
+        pool = ctx.enter_context(tc.tile_pool(name="held", bufs=1))
+        psum = ctx.enter_context(tc.psum_pool(name="psum", bufs=1))
+
+        def sb(name, cols, dtype=F32, over=None):
+            return pool.tile([P, cols], dtype, name=name, tag=over or name, align_bytes=64)
+
+        token_list = pool.tile([P, SLOTS // 16], U16, name="token_list")
+        link_list = pool.tile([P, SLOTS // 16], U16, name="link_list")
+        kw = sb("kw", T, U16)
+        vw = sb("vw", T, U16)
+        ks = sb("ks", T, U8)
+        vs = sb("vs", T, U8)
+        q_raw = sb("q_raw", PACK * ROWS)
+        g_raw = sb("g_raw", PACK * ROWS)
+        res = sb("res", 1)
+        old_sb = sb("old_sb", T)
+        linked = sb("linked", SLOTS)
+        placed = sb("placed", T)
+
+        def half(h):
+            return slice(h * HALF, (h + 1) * HALF)
+
+        def list_half(lst, h):
+            return lst[:, h * LIST_COLS:(h + 1) * LIST_COLS]
+
+        def load_scales(eng, tile, scales):
+            for quad in range(4):
+                eng.dma_start(out=tile[32 * quad:32 * quad + 4, :].bitcast(I32), in_=scales[0, 4 * quad:4 * quad + 4, :].bitcast(I32))
+
+        nc.vector.memset(ks[:].bitcast(I32), 0)
+        nc.vector.memset(vs[:].bitcast(I32), 0)
+        nc.gpsimd.dma_start(out=res[:], in_=reserve)
+        nc.sync.dma_start(token_list[:], offs)
+        nc.sync.dma_start(out=kw[:].bitcast(I32), in_=keys_words[0].bitcast(I32))
+        nc.sync.dma_start(out=q_raw[:], in_=query.rearrange("(p j) w -> p (j w)", j=PACK))
+        load_scales(nc.sync, ks, keys_scales)
+        nc.sync.dma_start(out=g_raw[:], in_=gout.rearrange("(p j) w -> p (j w)", j=PACK))
+        nc.sync.dma_start(out=vw[:].bitcast(I32), in_=vals_words[0].bitcast(I32))
+        nc.sync.dma_start(link_list[:], offs2)
+        load_scales(nc.sync, vs, vals_scales)
+        nc.sync.dma_start(out=old_sb[:], in_=old)
+        nc.vector.memset(linked[:].bitcast(I32), 0)
+        nc.gpsimd.memset(placed[:].bitcast(I32), 0)
+
+        def cast(name, raw):
+            grouped = sb(name, PACK * ROWS, BF16)
+            nc.scalar.activation(grouped[:].rearrange("p (w j) -> p w j", j=PACK), raw[:].rearrange("p (j w) -> p w j", j=PACK), ACT.Copy)
+            return grouped
+
+        def quantise(name, grouped):
+            codes = sb(name + "_codes", ROWS, U32)
+            scales = sb(name + "_scales", ROWS, U8)
+            nc.vector.quantize_mx(out=codes[:].bitcast(FP8X4), scales=scales[:], in_=grouped[:])
+            return codes, scales
+
+        def gather(name, window, h, dtype, over=None):
+            picked = sb(name, HALF, dtype, over)
+            nc.vector.tensor_copy(picked[:], window[:].indirect(list_half(token_list, h)))
+            return picked
+
+        def product(name, rows, words, scales):
+            bank = psum.tile([P, HALF], F32, name=name)
+            nc.tensor.matmul_mx(out=bank[:], lhsT=rows[0][:].bitcast(FP8X4), lhsT_scale=rows[1][:], rhs=words.bitcast(FP4X4), rhs_scale=scales, start=True, stop=True)
+            return bank
+
+        q_bf = cast("q_bf", q_raw)
+        g_bf = cast("g_bf", g_raw)
+        p = sb("p", SLOTS)
+        p_res = [sb("p_res%d" % h, HALF) for h in range(2)]
+        z_part = [sb("z_part%d" % h, 1) for h in range(2)]
+        kw_g = [gather("kw_g%d" % h, kw, h, U16) for h in range(2)]
+        for h in range(2):
+            ks_g = gather("ks_g%d" % h, ks, h, U8)
+            if h == 0:
+                q_mx = quantise("q", q_bf)
+            a = product("a%d" % h, q_mx, kw_g[h][:], ks_g[:])
+            nc.scalar.activation(p[:, half(h)], a[:], ACT.Exp, accum_out=z_part[h][:])
+            nc.scalar.activation(p_res[h][:], p[:, half(h)], ACT.Identity, bias=res[:])
+
+        vw_g = sb("vw_g", SLOTS, U16, over="q_bf")
+        nc.vector.tensor_copy(vw_g[:], vw[:].indirect(token_list[:]))
+        g_mx = quantise("g", g_bf)
+        inv = []
+        for h in range(2):
+            den = sb("den%d" % h, HALF)
+            nc.vector.tensor_tensor(den[:], p[:].indirect(list_half(link_list, h)), p_res[h][:], ALU.add)
+            root = sb("root%d" % h, HALF)
+            nc.scalar.activation(root[:], den[:], ACT.Abs_reciprocal_sqrt)
+            inv_h = sb("inv%d" % h, HALF)
+            nc.scalar.activation(inv_h[:], root[:], ACT.Square)
+            inv.append(inv_h)
+        neg_z = sb("neg_z", 1)
+        nc.vector.tensor_scalar(neg_z[:], z_part[0][:], z_part[1][:], -1.0, ALU.add, ALU.mult)
+        vs_g = sb("vs_g", SLOTS, U8, over="p_res0")
+        nc.vector.tensor_copy(vs_g[:], vs[:].indirect(token_list[:]))
+        neg_rz = sb("neg_rz", 1)
+        nc.vector.reciprocal(neg_rz[:], neg_z[:])
+
+        u = sb("u", SLOTS)
+        e1 = sb("e1", SLOTS)
+        p_gain = sb("p_gain", SLOTS, over="inv0")
+        for h in range(2):
+            c = product("c%d" % h, g_mx, vw_g[:, half(h)], vs_g[:, half(h)])
+            r = sb("r%d" % h, HALF, over=("vs", "r1")[h])
+            nc.vector.tensor_tensor(r[:], p[:, half(h)], inv[h][:], ALU.mult)
+            if h == 0:
+                nc.vector.tensor_scalar(p_gain[:], p[:], GAIN, None, ALU.mult)
+            nc.vector.scalar_tensor_tensor(u[:, half(h)], c[:], neg_rz[:], r[:], ALU.mult, ALU.mult)
+            nc.vector.tensor_tensor(e1[:, half(h)], u[:, half(h)], r[:], ALU.mult)
+            nc.scalar.activation(linked[:].indirect(list_half(link_list, h)), e1[:, half(h)], ACT.Copy)
+
+        terms = sb("terms", SLOTS)
+        neg_dz = sb("neg_dz", 1)
+        nc.vector.scalar_tensor_tensor(terms[:], u[:], neg_rz[:], p[:], ALU.mult, ALU.mult, accum_out=neg_dz[:])
+        own = sb("own", SLOTS)
+        nc.vector.scalar_tensor_tensor(own[:], u[:], -2.0, e1[:], ALU.mult, ALU.add)
+        dp = sb("dp", SLOTS)
+        nc.vector.scalar_tensor_tensor(dp[:], own[:], neg_dz[:], linked[:], ALU.subtract, ALU.add)
+        nc.vector.tensor_tensor(placed[:].indirect(token_list[:]), dp[:], p_gain[:], ALU.mult)
+
+        for n, width in enumerate(OUT_CHUNKS):
+            first = sum(OUT_CHUNKS[:n])
+            cols = slice(first, first + width)
+            result = sb("result%d" % n, width)
+            nc.vector.tensor_tensor(result[:], placed[:, cols], old_sb[:, cols], ALU.add)
+            (nc.sync if n % 2 == 0 else nc.scalar).dma_start(out=out[:, cols], in_=result[:])

@@ -55,12 +55,11 @@ def tile_attend_bneighbourshare_s_kernel(tc, query, keys_words, keys_scales, res
             return lst[:, h * LIST_COLS:(h + 1) * LIST_COLS]
 
         def load_scales(eng, tile, scales):
-            for quad in range(4):
-                eng.dma_start(out=tile[32 * quad:32 * quad + 4, :].bitcast(I32), in_=scales[0, 4 * quad:4 * quad + 4, :].bitcast(I32))
+            for row in range(4):
+                eng.dma_start(out=tile[row:P:32, :].bitcast(I32), in_=scales[0, row:16:4, :].bitcast(I32))
 
         nc.vector.memset(ks[:].bitcast(I32), 0)
         nc.vector.memset(vs[:].bitcast(I32), 0)
-        nc.gpsimd.dma_start(out=res[:], in_=reserve)
         nc.sync.dma_start(token_list[:], offs)
         nc.sync.dma_start(out=kw[:].bitcast(I32), in_=keys_words[0].bitcast(I32))
         nc.sync.dma_start(out=q_raw[:], in_=query.rearrange("(p j) w -> p (j w)", j=PACK))
@@ -68,14 +67,15 @@ def tile_attend_bneighbourshare_s_kernel(tc, query, keys_words, keys_scales, res
         nc.sync.dma_start(out=g_raw[:], in_=gout.rearrange("(p j) w -> p (j w)", j=PACK))
         nc.sync.dma_start(out=vw[:].bitcast(I32), in_=vals_words[0].bitcast(I32))
         nc.sync.dma_start(link_list[:], offs2)
+        nc.sync.dma_start(out=res[:], in_=reserve)
         load_scales(nc.sync, vs, vals_scales)
         nc.sync.dma_start(out=old_sb[:], in_=old)
         nc.vector.memset(linked[:].bitcast(I32), 0)
-        nc.gpsimd.memset(placed[:].bitcast(I32), 0)
+        nc.vector.memset(placed[:].bitcast(I32), 0)
 
         def cast(name, raw):
             grouped = sb(name, PACK * ROWS, BF16)
-            nc.scalar.activation(grouped[:].rearrange("p (w j) -> p w j", j=PACK), raw[:].rearrange("p (j w) -> p w j", j=PACK), ACT.Copy)
+            nc.scalar.activation(grouped[:].rearrange("p (c i j) -> p c j i", i=4, j=PACK), raw[:].rearrange("p (j c i) -> p c j i", j=PACK, i=4), ACT.Copy)
             return grouped
 
         def quantise(name, grouped):
@@ -106,7 +106,7 @@ def tile_attend_bneighbourshare_s_kernel(tc, query, keys_words, keys_scales, res
                 q_mx = quantise("q", q_bf)
             a = product("a%d" % h, q_mx, kw_g[h][:], ks_g[:])
             nc.scalar.activation(p[:, half(h)], a[:], ACT.Exp, accum_out=z_part[h][:])
-            nc.scalar.activation(p_res[h][:], p[:, half(h)], ACT.Identity, bias=res[:])
+            nc.scalar.activation(p_res[h][:], p[:, half(h)], ACT.Copy)
 
         vw_g = sb("vw_g", SLOTS, U16, over="q_bf")
         nc.vector.tensor_copy(vw_g[:], vw[:].indirect(token_list[:]))
@@ -116,7 +116,7 @@ def tile_attend_bneighbourshare_s_kernel(tc, query, keys_words, keys_scales, res
             den = sb("den%d" % h, HALF)
             nc.vector.tensor_tensor(den[:], p[:].indirect(list_half(link_list, h)), p_res[h][:], ALU.add)
             root = sb("root%d" % h, HALF)
-            nc.scalar.activation(root[:], den[:], ACT.Abs_reciprocal_sqrt)
+            nc.scalar.activation(root[:], den[:], ACT.Abs_reciprocal_sqrt, bias=res[:])
             inv_h = sb("inv%d" % h, HALF)
             nc.scalar.activation(inv_h[:], root[:], ACT.Square)
             inv.append(inv_h)
@@ -129,13 +129,10 @@ def tile_attend_bneighbourshare_s_kernel(tc, query, keys_words, keys_scales, res
 
         u = sb("u", SLOTS)
         e1 = sb("e1", SLOTS)
-        p_gain = sb("p_gain", SLOTS, over="inv0")
         for h in range(2):
             c = product("c%d" % h, g_mx, vw_g[:, half(h)], vs_g[:, half(h)])
             r = sb("r%d" % h, HALF, over=("vs", "r1")[h])
             nc.vector.tensor_tensor(r[:], p[:, half(h)], inv[h][:], ALU.mult)
-            if h == 0:
-                nc.vector.tensor_scalar(p_gain[:], p[:], GAIN, None, ALU.mult)
             nc.vector.scalar_tensor_tensor(u[:, half(h)], c[:], neg_rz[:], r[:], ALU.mult, ALU.mult)
             nc.vector.tensor_tensor(e1[:, half(h)], u[:, half(h)], r[:], ALU.mult)
             nc.scalar.activation(linked[:].indirect(list_half(link_list, h)), e1[:, half(h)], ACT.Copy)
@@ -145,6 +142,8 @@ def tile_attend_bneighbourshare_s_kernel(tc, query, keys_words, keys_scales, res
         nc.vector.scalar_tensor_tensor(terms[:], u[:], neg_rz[:], p[:], ALU.mult, ALU.mult, accum_out=neg_dz[:])
         own = sb("own", SLOTS)
         nc.vector.scalar_tensor_tensor(own[:], u[:], -2.0, e1[:], ALU.mult, ALU.add)
+        p_gain = sb("p_gain", SLOTS, over="r1")
+        nc.vector.tensor_scalar(p_gain[:], p[:], GAIN, None, ALU.mult)
         dp = sb("dp", SLOTS)
         nc.vector.scalar_tensor_tensor(dp[:], own[:], neg_dz[:], linked[:], ALU.subtract, ALU.add)
         nc.vector.tensor_tensor(placed[:].indirect(token_list[:]), dp[:], p_gain[:], ALU.mult)

@@ -21,7 +21,8 @@ ROWS = 128
 HALF = SLOTS // 2
 LIST_COLS = HALF // 16
 GAIN = 512.0
-OUT_CHUNKS = (640, 640, 512, 256)
+SCALAR_SLOTS = 416
+OUT_CHUNKS = (512, 512, 512, 512)
 
 FLOPS = 2 * 2 * 512 * ROWS * SLOTS
 
@@ -46,7 +47,7 @@ def tile_attend_bneighbourshare_s_kernel(tc, query, keys_words, keys_scales, res
         res = sb("res", 1)
         old_sb = sb("old_sb", T)
         linked = sb("linked", SLOTS)
-        placed = sb("placed", T)
+        linked_rest = sb("linked_rest", SLOTS)
 
         def half(h):
             return slice(h * HALF, (h + 1) * HALF)
@@ -60,18 +61,18 @@ def tile_attend_bneighbourshare_s_kernel(tc, query, keys_words, keys_scales, res
 
         nc.vector.memset(ks[:].bitcast(I32), 0)
         nc.vector.memset(vs[:].bitcast(I32), 0)
-        nc.sync.dma_start(token_list[:], offs)
         nc.sync.dma_start(out=kw[:].bitcast(I32), in_=keys_words[0].bitcast(I32))
+        nc.sync.dma_start(token_list[:], offs)
         nc.sync.dma_start(out=q_raw[:], in_=query.rearrange("(p j) w -> p (j w)", j=PACK))
         load_scales(nc.sync, ks, keys_scales)
         nc.sync.dma_start(out=g_raw[:], in_=gout.rearrange("(p j) w -> p (j w)", j=PACK))
         nc.sync.dma_start(out=vw[:].bitcast(I32), in_=vals_words[0].bitcast(I32))
         nc.sync.dma_start(link_list[:], offs2)
-        nc.sync.dma_start(out=res[:], in_=reserve)
         load_scales(nc.sync, vs, vals_scales)
+        nc.sync.dma_start(out=res[:], in_=reserve)
         nc.sync.dma_start(out=old_sb[:], in_=old)
         nc.vector.memset(linked[:].bitcast(I32), 0)
-        nc.vector.memset(placed[:].bitcast(I32), 0)
+        nc.vector.memset(linked_rest[:].bitcast(I32), 0)
 
         def cast(name, raw):
             grouped = sb(name, PACK * ROWS, BF16)
@@ -122,30 +123,35 @@ def tile_attend_bneighbourshare_s_kernel(tc, query, keys_words, keys_scales, res
             inv.append(inv_h)
         neg_z = sb("neg_z", 1)
         nc.vector.tensor_scalar(neg_z[:], z_part[0][:], z_part[1][:], -1.0, ALU.add, ALU.mult)
-        vs_g = sb("vs_g", SLOTS, U8, over="p_res0")
-        nc.vector.tensor_copy(vs_g[:], vs[:].indirect(token_list[:]))
+        vs_g = [gather("vs_g%d" % h, vs, h, U8, over="p_res%d" % h) for h in range(2)]
         neg_rz = sb("neg_rz", 1)
         nc.vector.reciprocal(neg_rz[:], neg_z[:])
+        p_gain = sb("p_gain", SLOTS, over="root1")
+        nc.scalar.activation(p_gain[:], p[:], ACT.Copy, scale=GAIN)
 
+        c = [product("c%d" % h, g_mx, vw_g[:, half(h)], vs_g[h][:]) for h in range(2)]
+        r = sb("r", SLOTS)
         u = sb("u", SLOTS)
-        e1 = sb("e1", SLOTS)
+        e1 = sb("e1", SCALAR_SLOTS)
         for h in range(2):
-            c = product("c%d" % h, g_mx, vw_g[:, half(h)], vs_g[:, half(h)])
-            r = sb("r%d" % h, HALF, over=("vs", "r1")[h])
-            nc.vector.tensor_tensor(r[:], p[:, half(h)], inv[h][:], ALU.mult)
-            nc.vector.scalar_tensor_tensor(u[:, half(h)], c[:], neg_rz[:], r[:], ALU.mult, ALU.mult)
-            nc.vector.tensor_tensor(e1[:, half(h)], u[:, half(h)], r[:], ALU.mult)
-            nc.scalar.activation(linked[:].indirect(list_half(link_list, h)), e1[:, half(h)], ACT.Copy)
+            nc.vector.tensor_tensor(r[:, half(h)], p[:, half(h)], inv[h][:], ALU.mult)
+            nc.vector.scalar_tensor_tensor(u[:, half(h)], c[h][:], neg_rz[:], r[:, half(h)], ALU.mult, ALU.mult)
+            part = slice(h * HALF, min((h + 1) * HALF, SCALAR_SLOTS))
+            nc.vector.tensor_tensor(e1[:, part], u[:, part], r[:, part], ALU.mult)
+            nc.scalar.activation(linked[:].indirect(link_list[:, part.start // 16:part.stop // 16]), e1[:, part], ACT.Copy)
+        nc.vector.tensor_tensor(linked_rest[:].indirect(link_list[:, SCALAR_SLOTS // 16:]), u[:, SCALAR_SLOTS:], r[:, SCALAR_SLOTS:], ALU.mult)
+        placed = sb("placed", T, over="inv0")
+        nc.gpsimd.memset(placed[:].bitcast(I32), 0)
 
         terms = sb("terms", SLOTS)
         neg_dz = sb("neg_dz", 1)
         nc.vector.scalar_tensor_tensor(terms[:], u[:], neg_rz[:], p[:], ALU.mult, ALU.mult, accum_out=neg_dz[:])
         own = sb("own", SLOTS)
-        nc.vector.scalar_tensor_tensor(own[:], u[:], -2.0, e1[:], ALU.mult, ALU.add)
-        p_gain = sb("p_gain", SLOTS, over="r1")
-        nc.vector.tensor_scalar(p_gain[:], p[:], GAIN, None, ALU.mult)
+        nc.vector.scalar_tensor_tensor(own[:], r[:], -2.0, u[:], ALU.add, ALU.mult)
+        partial = sb("partial", SLOTS)
+        nc.vector.scalar_tensor_tensor(partial[:], own[:], neg_dz[:], linked_rest[:], ALU.subtract, ALU.add)
         dp = sb("dp", SLOTS)
-        nc.vector.scalar_tensor_tensor(dp[:], own[:], neg_dz[:], linked[:], ALU.subtract, ALU.add)
+        nc.vector.tensor_tensor(dp[:], partial[:], linked[:], ALU.add)
         nc.vector.tensor_tensor(placed[:].indirect(token_list[:]), dp[:], p_gain[:], ALU.mult)
 
         for n, width in enumerate(OUT_CHUNKS):

@@ -21,8 +21,8 @@ ROWS = 128
 HALF = SLOTS // 2
 LIST_COLS = HALF // 16
 GAIN = 512.0
-SCALAR_SLOTS = 416
-OUT_CHUNKS = (512, 512, 512, 512)
+SCALAR_SLOTS = 384
+OUT_CHUNKS = (512, 512, 512, 256, 256)
 
 FLOPS = 2 * 2 * 512 * ROWS * SLOTS
 
@@ -61,8 +61,8 @@ def tile_attend_bneighbourshare_s_kernel(tc, query, keys_words, keys_scales, res
 
         nc.vector.memset(ks[:].bitcast(I32), 0)
         nc.vector.memset(vs[:].bitcast(I32), 0)
-        nc.sync.dma_start(out=kw[:].bitcast(I32), in_=keys_words[0].bitcast(I32))
         nc.sync.dma_start(token_list[:], offs)
+        nc.sync.dma_start(out=kw[:].bitcast(I32), in_=keys_words[0].bitcast(I32))
         nc.sync.dma_start(out=q_raw[:], in_=query.rearrange("(p j) w -> p (j w)", j=PACK))
         load_scales(nc.sync, ks, keys_scales)
         nc.sync.dma_start(out=g_raw[:], in_=gout.rearrange("(p j) w -> p (j w)", j=PACK))
@@ -107,20 +107,21 @@ def tile_attend_bneighbourshare_s_kernel(tc, query, keys_words, keys_scales, res
                 q_mx = quantise("q", q_bf)
             a = product("a%d" % h, q_mx, kw_g[h][:], ks_g[:])
             nc.scalar.activation(p[:, half(h)], a[:], ACT.Exp, accum_out=z_part[h][:])
-            nc.scalar.activation(p_res[h][:], p[:, half(h)], ACT.Copy)
+            nc.scalar.activation(p_res[h][:], a[:], ACT.Exp, scale=-1.0)
 
         vw_g = sb("vw_g", SLOTS, U16, over="q_bf")
         nc.vector.tensor_copy(vw_g[:], vw[:].indirect(token_list[:]))
         g_mx = quantise("g", g_bf)
-        inv = []
+        p_link = [sb("p_link%d" % h, HALF) for h in range(2)]
         for h in range(2):
-            den = sb("den%d" % h, HALF)
-            nc.vector.tensor_tensor(den[:], p[:].indirect(list_half(link_list, h)), p_res[h][:], ALU.add)
+            nc.vector.tensor_copy(p_link[h][:], p[:].indirect(list_half(link_list, h)))
+        r = sb("r", SLOTS)
+        for h in range(2):
+            ratio = sb("ratio%d" % h, HALF)
+            nc.vector.scalar_tensor_tensor(ratio[:], p_link[h][:], res[:], p_res[h][:], ALU.add, ALU.mult)
             root = sb("root%d" % h, HALF)
-            nc.scalar.activation(root[:], den[:], ACT.Abs_reciprocal_sqrt, bias=res[:])
-            inv_h = sb("inv%d" % h, HALF)
-            nc.scalar.activation(inv_h[:], root[:], ACT.Square)
-            inv.append(inv_h)
+            nc.scalar.activation(root[:], ratio[:], ACT.Abs_reciprocal_sqrt, bias=1.0)
+            nc.scalar.activation(r[:, half(h)], root[:], ACT.Square)
         neg_z = sb("neg_z", 1)
         nc.vector.tensor_scalar(neg_z[:], z_part[0][:], z_part[1][:], -1.0, ALU.add, ALU.mult)
         vs_g = [gather("vs_g%d" % h, vs, h, U8, over="p_res%d" % h) for h in range(2)]
@@ -130,28 +131,30 @@ def tile_attend_bneighbourshare_s_kernel(tc, query, keys_words, keys_scales, res
         nc.scalar.activation(p_gain[:], p[:], ACT.Copy, scale=GAIN)
 
         c = [product("c%d" % h, g_mx, vw_g[:, half(h)], vs_g[h][:]) for h in range(2)]
-        r = sb("r", SLOTS)
         u = sb("u", SLOTS)
         e1 = sb("e1", SCALAR_SLOTS)
         for h in range(2):
-            nc.vector.tensor_tensor(r[:, half(h)], p[:, half(h)], inv[h][:], ALU.mult)
             nc.vector.scalar_tensor_tensor(u[:, half(h)], c[h][:], neg_rz[:], r[:, half(h)], ALU.mult, ALU.mult)
             part = slice(h * HALF, min((h + 1) * HALF, SCALAR_SLOTS))
             nc.vector.tensor_tensor(e1[:, part], u[:, part], r[:, part], ALU.mult)
-            nc.scalar.activation(linked[:].indirect(link_list[:, part.start // 16:part.stop // 16]), e1[:, part], ACT.Copy)
-        nc.vector.tensor_tensor(linked_rest[:].indirect(link_list[:, SCALAR_SLOTS // 16:]), u[:, SCALAR_SLOTS:], r[:, SCALAR_SLOTS:], ALU.mult)
-        placed = sb("placed", T, over="inv0")
+        nc.scalar.activation(linked_rest[:].indirect(list_half(link_list, 0)), e1[:, half(0)], ACT.Copy)
+        nc.vector.tensor_tensor(linked[:].indirect(link_list[:, SCALAR_SLOTS // 16:]), u[:, SCALAR_SLOTS:], r[:, SCALAR_SLOTS:], ALU.mult)
+        nc.scalar.activation(linked[:].indirect(link_list[:, LIST_COLS:SCALAR_SLOTS // 16]), e1[:, HALF:], ACT.Copy)
+        placed = sb("placed", T, over="p_res0")
         nc.gpsimd.memset(placed[:].bitcast(I32), 0)
 
         terms = sb("terms", SLOTS)
         neg_dz = sb("neg_dz", 1)
         nc.vector.scalar_tensor_tensor(terms[:], u[:], neg_rz[:], p[:], ALU.mult, ALU.mult, accum_out=neg_dz[:])
         own = sb("own", SLOTS)
-        nc.vector.scalar_tensor_tensor(own[:], r[:], -2.0, u[:], ALU.add, ALU.mult)
         partial = sb("partial", SLOTS)
-        nc.vector.scalar_tensor_tensor(partial[:], own[:], neg_dz[:], linked_rest[:], ALU.subtract, ALU.add)
         dp = sb("dp", SLOTS)
-        nc.vector.tensor_tensor(dp[:], partial[:], linked[:], ALU.add)
+        for h in range(2):
+            nc.vector.scalar_tensor_tensor(own[:, half(h)], r[:, half(h)], -2.0, u[:, half(h)], ALU.add, ALU.mult)
+        for h in range(2):
+            nc.vector.scalar_tensor_tensor(partial[:, half(h)], own[:, half(h)], neg_dz[:], linked_rest[:, half(h)], ALU.subtract, ALU.add)
+        for h in range(2):
+            nc.vector.tensor_tensor(dp[:, half(h)], partial[:, half(h)], linked[:, half(h)], ALU.add)
         nc.vector.tensor_tensor(placed[:].indirect(token_list[:]), dp[:], p_gain[:], ALU.mult)
 
         for n, width in enumerate(OUT_CHUNKS):

@@ -22,7 +22,7 @@ HALF = SLOTS // 2
 LIST_COLS = HALF // 16
 GAIN = 512.0
 SCALAR_SLOTS = 384
-OUT_CHUNKS = (512, 512, 512, 256, 256)
+OUT_CHUNKS = (256, 512, 512, 512, 256)
 
 FLOPS = 2 * 2 * 512 * ROWS * SLOTS
 
@@ -48,6 +48,7 @@ def tile_attend_bneighbourshare_s_kernel(tc, query, keys_words, keys_scales, res
         old_sb = sb("old_sb", T)
         linked = sb("linked", SLOTS)
         linked_rest = sb("linked_rest", SLOTS)
+        placed = sb("placed", T)
 
         def half(h):
             return slice(h * HALF, (h + 1) * HALF)
@@ -73,6 +74,7 @@ def tile_attend_bneighbourshare_s_kernel(tc, query, keys_words, keys_scales, res
         nc.sync.dma_start(out=old_sb[:], in_=old)
         nc.vector.memset(linked[:].bitcast(I32), 0)
         nc.vector.memset(linked_rest[:].bitcast(I32), 0)
+        nc.vector.memset(placed[:].bitcast(I32), 0)
 
         def cast(name, raw):
             grouped = sb(name, PACK * ROWS, BF16)
@@ -140,8 +142,6 @@ def tile_attend_bneighbourshare_s_kernel(tc, query, keys_words, keys_scales, res
         nc.scalar.activation(linked_rest[:].indirect(list_half(link_list, 0)), e1[:, half(0)], ACT.Copy)
         nc.vector.tensor_tensor(linked[:].indirect(link_list[:, SCALAR_SLOTS // 16:]), u[:, SCALAR_SLOTS:], r[:, SCALAR_SLOTS:], ALU.mult)
         nc.scalar.activation(linked[:].indirect(link_list[:, LIST_COLS:SCALAR_SLOTS // 16]), e1[:, HALF:], ACT.Copy)
-        placed = sb("placed", T, over="p_res0")
-        nc.gpsimd.memset(placed[:].bitcast(I32), 0)
 
         terms = sb("terms", SLOTS)
         neg_dz = sb("neg_dz", 1)

from contextlib import ExitStack

import concourse.mybir as mybir

F32 = mybir.dt.float32
BF16 = mybir.dt.bfloat16
I32 = mybir.dt.int32
U32 = mybir.dt.uint32
U16 = mybir.dt.uint16
U8 = mybir.dt.uint8
FP8X4 = mybir.dt.float8_e4m3fn_x4
FP4X4 = mybir.dt.float4_e2m1fn_x4
ALU = mybir.AluOpType
ACT = mybir.ActivationFunctionType

P = 128
PACK = 4
T = 2048
SLOTS = 512
ROWS = 128
HALF = SLOTS // 2
LIST_COLS = HALF // 16
GAIN = 512.0
SCALAR_SLOTS = 384
OUT_CHUNKS = (256, 512, 512, 512, 256)

FLOPS = 2 * 2 * 512 * ROWS * SLOTS


def tile_attend_bneighbourshare_s_kernel(tc, query, keys_words, keys_scales, reserve, gout, vals_words, vals_scales, old, offs2, offs, out):
    nc = tc.nc
    with ExitStack() as ctx:
        pool = ctx.enter_context(tc.tile_pool(name="held", bufs=1))
        psum = ctx.enter_context(tc.psum_pool(name="psum", bufs=1))

        def sb(name, cols, dtype=F32, over=None):
            return pool.tile([P, cols], dtype, name=name, tag=over or name, align_bytes=64)

        token_list = pool.tile([P, SLOTS // 16], U16, name="token_list")
        link_list = pool.tile([P, SLOTS // 16], U16, name="link_list")
        kw = sb("kw", T, U16)
        vw = sb("vw", T, U16)
        ks = sb("ks", T, U8)
        vs = sb("vs", T, U8)
        q_raw = sb("q_raw", PACK * ROWS)
        g_raw = sb("g_raw", PACK * ROWS)
        res = sb("res", 1)
        old_sb = sb("old_sb", T)
        linked = sb("linked", SLOTS)
        linked_rest = sb("linked_rest", SLOTS)
        placed = sb("placed", T)

        def half(h):
            return slice(h * HALF, (h + 1) * HALF)

        def list_half(lst, h):
            return lst[:, h * LIST_COLS:(h + 1) * LIST_COLS]

        def load_scales(eng, tile, scales):
            for row in range(4):
                eng.dma_start(out=tile[row:P:32, :].bitcast(I32), in_=scales[0, row:16:4, :].bitcast(I32))

        nc.vector.memset(ks[:].bitcast(I32), 0)
        nc.vector.memset(vs[:].bitcast(I32), 0)
        nc.sync.dma_start(token_list[:], offs)
        nc.sync.dma_start(out=kw[:].bitcast(I32), in_=keys_words[0].bitcast(I32))
        nc.sync.dma_start(out=q_raw[:], in_=query.rearrange("(p j) w -> p (j w)", j=PACK))
        load_scales(nc.sync, ks, keys_scales)
        nc.sync.dma_start(out=g_raw[:], in_=gout.rearrange("(p j) w -> p (j w)", j=PACK))
        nc.sync.dma_start(out=vw[:].bitcast(I32), in_=vals_words[0].bitcast(I32))
        nc.sync.dma_start(link_list[:], offs2)
        load_scales(nc.sync, vs, vals_scales)
        nc.sync.dma_start(out=res[:], in_=reserve)
        nc.sync.dma_start(out=old_sb[:], in_=old)
        nc.vector.memset(linked[:].bitcast(I32), 0)
        nc.vector.memset(linked_rest[:].bitcast(I32), 0)
        nc.vector.memset(placed[:].bitcast(I32), 0)

        def cast(name, raw):
            grouped = sb(name, PACK * ROWS, BF16)
            nc.scalar.activation(grouped[:].rearrange("p (c i j) -> p c j i", i=4, j=PACK), raw[:].rearrange("p (j c i) -> p c j i", j=PACK, i=4), ACT.Copy)
            return grouped

        def quantise(name, grouped):
            codes = sb(name + "_codes", ROWS, U32)
            scales = sb(name + "_scales", ROWS, U8)
            nc.vector.quantize_mx(out=codes[:].bitcast(FP8X4), scales=scales[:], in_=grouped[:])
            return codes, scales

        def gather(name, window, h, dtype, over=None):
            picked = sb(name, HALF, dtype, over)
            nc.vector.tensor_copy(picked[:], window[:].indirect(list_half(token_list, h)))
            return picked

        def product(name, rows, words, scales):
            bank = psum.tile([P, HALF], F32, name=name)
            nc.tensor.matmul_mx(out=bank[:], lhsT=rows[0][:].bitcast(FP8X4), lhsT_scale=rows[1][:], rhs=words.bitcast(FP4X4), rhs_scale=scales, start=True, stop=True)
            return bank

        q_bf = cast("q_bf", q_raw)
        g_bf = cast("g_bf", g_raw)
        p = sb("p", SLOTS)
        p_res = [sb("p_res%d" % h, HALF) for h in range(2)]
        z_part = [sb("z_part%d" % h, 1) for h in range(2)]
        kw_g = [gather("kw_g%d" % h, kw, h, U16) for h in range(2)]
        for h in range(2):
            ks_g = gather("ks_g%d" % h, ks, h, U8)
            if h == 0:
                q_mx = quantise("q", q_bf)
            a = product("a%d" % h, q_mx, kw_g[h][:], ks_g[:])
            nc.scalar.activation(p[:, half(h)], a[:], ACT.Exp, accum_out=z_part[h][:])
            nc.scalar.activation(p_res[h][:], a[:], ACT.Exp, scale=-1.0)

        vw_g = sb("vw_g", SLOTS, U16, over="q_bf")
        nc.vector.tensor_copy(vw_g[:], vw[:].indirect(token_list[:]))
        g_mx = quantise("g", g_bf)
        p_link = [sb("p_link%d" % h, HALF) for h in range(2)]
        for h in range(2):
            nc.vector.tensor_copy(p_link[h][:], p[:].indirect(list_half(link_list, h)))
        r = sb("r", SLOTS)
        for h in range(2):
            ratio = sb("ratio%d" % h, HALF)
            nc.vector.scalar_tensor_tensor(ratio[:], p_link[h][:], res[:], p_res[h][:], ALU.add, ALU.mult)
            root = sb("root%d" % h, HALF)
            nc.scalar.activation(root[:], ratio[:], ACT.Abs_reciprocal_sqrt, bias=1.0)
            nc.scalar.activation(r[:, half(h)], root[:], ACT.Square)
        neg_z = sb("neg_z", 1)
        nc.vector.tensor_scalar(neg_z[:], z_part[0][:], z_part[1][:], -1.0, ALU.add, ALU.mult)
        vs_g = [gather("vs_g%d" % h, vs, h, U8, over="p_res%d" % h) for h in range(2)]
        neg_rz = sb("neg_rz", 1)
        nc.vector.reciprocal(neg_rz[:], neg_z[:])
        p_gain = sb("p_gain", SLOTS, over="root1")
        nc.scalar.activation(p_gain[:], p[:], ACT.Copy, scale=GAIN)

        c = [product("c%d" % h, g_mx, vw_g[:, half(h)], vs_g[h][:]) for h in range(2)]
        u = sb("u", SLOTS)
        e1 = sb("e1", SCALAR_SLOTS)
        for h in range(2):
            nc.vector.scalar_tensor_tensor(u[:, half(h)], c[h][:], neg_rz[:], r[:, half(h)], ALU.mult, ALU.mult)
            part = slice(h * HALF, min((h + 1) * HALF, SCALAR_SLOTS))
            nc.vector.tensor_tensor(e1[:, part], u[:, part], r[:, part], ALU.mult)
        nc.scalar.activation(linked_rest[:].indirect(list_half(link_list, 0)), e1[:, half(0)], ACT.Copy)
        nc.vector.tensor_tensor(linked[:].indirect(link_list[:, SCALAR_SLOTS // 16:]), u[:, SCALAR_SLOTS:], r[:, SCALAR_SLOTS:], ALU.mult)
        nc.scalar.activation(linked[:].indirect(link_list[:, LIST_COLS:SCALAR_SLOTS // 16]), e1[:, HALF:], ACT.Copy)

        terms = sb("terms", SLOTS)
        neg_dz = sb("neg_dz", 1)
        nc.vector.scalar_tensor_tensor(terms[:], u[:], neg_rz[:], p[:], ALU.mult, ALU.mult, accum_out=neg_dz[:])
        own = sb("own", SLOTS)
        partial = sb("partial", SLOTS)
        dp = sb("dp", SLOTS)
        for h in range(2):
            nc.vector.scalar_tensor_tensor(own[:, half(h)], r[:, half(h)], -2.0, u[:, half(h)], ALU.add, ALU.mult)
        for h in range(2):
            nc.vector.scalar_tensor_tensor(partial[:, half(h)], own[:, half(h)], neg_dz[:], linked_rest[:, half(h)], ALU.subtract, ALU.add)
        for h in range(2):
            nc.vector.tensor_tensor(dp[:, half(h)], partial[:, half(h)], linked[:, half(h)], ALU.add)
        nc.vector.tensor_tensor(placed[:].indirect(token_list[:]), dp[:], p_gain[:], ALU.mult)

        for n, width in enumerate(OUT_CHUNKS):
            first = sum(OUT_CHUNKS[:n])
            cols = slice(first, first + width)
            result = sb("result%d" % n, width)
            nc.vector.tensor_tensor(result[:], placed[:, cols], old_sb[:, cols], ALU.add)
            (nc.sync if n % 2 == 0 else nc.scalar).dma_start(out=out[:, cols], in_=result[:])
